import numpy as np
import ml_dtypes


def mxq(x, axis, fmt="e4m3"):
    dtype, down = {"e4m3": (ml_dtypes.float8_e4m3fn, 7), "e5m2": (ml_dtypes.float8_e5m2, 14)}[fmt]
    v = np.moveaxis(np.asarray(x, np.float32).astype(ml_dtypes.bfloat16).astype(np.float64), axis, -1)
    blocks = v.reshape(v.shape[:-1] + (-1, 32))
    amax = np.abs(blocks).max(-1, keepdims=True)
    byte = np.maximum(np.where(amax > 0, np.frexp(amax)[1] - 1 + 127, 0) - down, 1)
    scale = np.exp2(byte - 127.0)
    codes = (blocks / scale).astype(np.float32).astype(dtype).astype(np.float64)
    return np.moveaxis((codes * scale).reshape(v.shape), -1, axis)


WIDE = False


def mx_kscale(k, group=512):
    if not WIDE:
        return np.ones(k)
    levels = np.array([10, -10, 5, -5, 0])
    if group != 512:
        return np.exp2(np.random.permutation(np.resize(levels, k // group))).repeat(group)
    if k % 512:
        return np.exp2(np.random.permutation(np.resize(levels, k // 32))).repeat(32)
    a = np.empty((k // 512, 16))
    for p in range(k // 512):
        a[p, :8] = np.random.permutation(np.resize(levels, 8))
        for g in range(8):
            far = levels[np.abs(levels - a[p, g]) >= 10]
            a[p, g + 8] = far[np.random.randint(len(far))]
    return np.exp2(a.ravel()).repeat(32)


def f64(x):
    return np.asarray(x).astype(np.float64)


def striped(idx):
    return np.tile(np.asarray(idx).reshape(-1, 16).T, (8, 1)).astype(np.uint16)


def unstriped(offs):
    return offs[:16].T.reshape(-1).astype(np.int64)


H, KV, D, NQ, N = 4, 2, 256, 512, 512
CAP = 2.0


def setup_inputs():
    n = np.random.standard_normal
    s = mx_kscale(D, 0)[:, None]
    u = mx_kscale(N)
    t = np.random.uniform(0.5, 2.0, N) * u
    v = n((KV, N, 128))
    return {
        "qT": (n((H, D, NQ)) * s * (0.70 / np.sqrt(D))).astype(np.float32),
        "kT": (n((KV, D, N)) / s).astype(np.float32),
        "t": t.reshape(N, 1).astype(np.float32),
        "v": (v / t[:, None]).astype(np.float32),
        "og": n((H, NQ, 128)).astype(np.float32),
    }


def reference(qT, kT, t, v, og):
    a = np.repeat(mxq(f64(kT), 1, "e4m3"), H // KV, 0).transpose(0, 2, 1) @ mxq(f64(qT), 1, "e4m3")
    a = CAP * np.tanh(a / CAP)
    p = 1.0 / (1.0 + np.exp(-a))
    w = p * f64(t)
    y = mxq(w, 1, "e4m3").transpose(0, 2, 1) @ np.repeat(mxq(f64(v), 1, "e4m3"), H // KV, 0)
    y = y / 16.0
    y = y / (1.0 + np.exp(-f64(og)))
    return y

@@ -1,0 +1,231 @@
+from contextlib import ExitStack
+
+import concourse.mybir as mybir
+
+H, KV, D, NQ, N, E = 4, 2, 256, 512, 512, 128
+CAP = 2.0
+FLOPS = 2 * H * N * NQ * D + 2 * H * N * NQ * E
+
+F32 = mybir.dt.float32
+BF16 = mybir.dt.bfloat16
+U32 = mybir.dt.uint32
+U8 = mybir.dt.uint8
+FP8X4 = mybir.dt.float8_e4m3fn_x4
+ACT = mybir.ActivationFunctionType
+ALU = mybir.AluOpType
+
+P = 128
+PACK = 4
+ROWS = D // PACK
+QT = 128
+TILES = NQ // QT
+HEAD_SETS = ((1, 2), (0, 3))
+PAIRS = len(HEAD_SETS) * TILES
+UNITS = KV * PAIRS
+
+
+def tile_rows_a_sigmoid_cap_gate_kernel(tc, qT, kT, t, v, og, out):
+    nc = tc.nc
+    with ExitStack() as ctx:
+        sb = ctx.enter_context(tc.tile_pool(name="sb", bufs=1))
+        ps = ctx.enter_context(tc.psum_pool(name="ps", bufs=1))
+        ctx.enter_context(tc.manual_schedule())
+
+        def tiles(pool, name, count, shape, dtype):
+            return [pool.tile(shape, dtype, name="%s%d" % (name, i), align_bytes=64) for i in range(count)]
+
+        def banks(name, count, shape):
+            return [ps.tile(shape, F32, name="%s%d" % (name, i)) for i in range(count)]
+
+        half = N // 2
+        k_raw = tiles(sb, "k_raw", 2, [P, PACK, half], F32)
+        k_bf = tiles(sb, "k_bf", 2, [P, PACK, half // PACK, PACK], BF16)
+        k_codes = sb.tile([P, PACK, P], U32, align_bytes=64)
+        k_scales = sb.tile([P, PACK, P], U8, align_bytes=64)
+        q_one = tiles(sb, "q_one", 2, [P, PACK, QT], F32)
+        q_two = tiles(sb, "q_two", 3, [P, PACK, 2 * QT], F32)
+        q_bf = tiles(sb, "q_bf", PAIRS, [P, QT, PACK], BF16)
+        q_codes = tiles(sb, "q_codes", PAIRS, [P, QT], U32)
+        q_scales = tiles(sb, "q_scales", PAIRS, [P, QT], U8)
+        v_raw = sb.tile([P, KV, PACK, E], F32, align_bytes=64)
+        v_bf = sb.tile([P, KV, E, PACK], BF16, align_bytes=64)
+        v_codes = sb.tile([P, KV, E], U32, align_bytes=64)
+        v_scales = sb.tile([P, KV, E], U8, align_bytes=64)
+        t_sb = sb.tile([P, PACK], F32, align_bytes=64)
+        og_first = sb.tile([P, KV, E], F32, align_bytes=64)
+        og_a = sb.tile([P, KV, TILES - 1, E], F32, align_bytes=64)
+        og_b = sb.tile([P, KV, TILES, E], F32, align_bytes=64)
+        gate = tiles(sb, "gate", PAIRS, [P, KV, E], F32)
+        capped = tiles(sb, "capped", UNITS, [P, QT, PACK], F32)
+        prob = tiles(sb, "prob", UNITS, [P, QT, PACK], F32)
+        w_bf = tiles(sb, "w_bf", UNITS, [P, QT, PACK], BF16)
+        w_codes = tiles(sb, "w_codes", UNITS, [P, QT], U32)
+        w_scales = tiles(sb, "w_scales", UNITS, [P, QT], U8)
+        result = tiles(sb, "result", PAIRS, [P, KV, E], F32)
+        scores = [banks("scores%d_" % g, 2, [P, PACK, QT]) for g in range(KV)]
+        y_banks = banks("y", 4, [P, 2, KV, E])
+
+        k_hbm = kT.rearrange("g (p j) n -> (g p) j n", j=PACK)
+        q_hbm = qT.rearrange("h (p j) n -> (h p) j n", j=PACK)
+        q_a = q_hbm[ROWS : 3 * ROWS]
+        og_hbm = og.rearrange("h (c p) e -> p h c e", p=P)
+        out_hbm = out.rearrange("h (c p) e -> p h c e", p=P)
+        nc.sync.dma_start(out=og_first[:], in_=og_hbm[:, 1:3, 0, :])
+        for h in range(2):
+            nc.sync.dma_start(out=k_raw[h][:], in_=k_hbm[:, :, half * h : half * (h + 1)])
+        for c in range(2):
+            nc.sync.dma_start(out=q_one[c][:], in_=q_a[:, :, QT * c : QT * (c + 1)])
+        nc.sync.dma_start(out=t_sb[:], in_=t.rearrange("(p j) o -> p (j o)", j=PACK))
+        nc.sync.dma_start(out=v_raw[:], in_=v.rearrange("g (p j) e -> p g j e", j=PACK))
+        nc.sync.dma_start(out=q_two[0][:], in_=q_a[:, :, 2 * QT :])
+        for g in range(KV):
+            nc.sync.dma_start(out=og_a[:, g], in_=og_hbm[:, HEAD_SETS[0][g], 1:, :])
+        for c in range(2):
+            for g in range(KV):
+                head = HEAD_SETS[1][g]
+                nc.sync.dma_start(
+                    out=q_two[1 + c][ROWS * g : ROWS * (g + 1)],
+                    in_=q_hbm[ROWS * head : ROWS * (head + 1), :, 2 * QT * c : 2 * QT * (c + 1)],
+                )
+        for g in range(KV):
+            nc.sync.dma_start(out=og_b[:, g], in_=og_hbm[:, HEAD_SETS[1][g], :, :])
+
+        def q_source(i):
+            if i < 2:
+                return q_one[i][:]
+            return q_two[i // 2 - 1][:, :, QT * (i % 2) : QT * (i % 2 + 1)]
+
+        def og_source(i):
+            if i == 0:
+                return og_first[:]
+            if i < TILES:
+                return og_a[:, :, i - 1, :]
+            return og_b[:, :, i - TILES, :]
+
+        def interleave(copy, dst, src):
+            copy(out=dst.rearrange("p (c i) j -> p c j i", i=4), in_=src.rearrange("p j (c i) -> p c j i", i=4))
+
+        def quantize(codes, scales, values):
+            nc.vector.quantize_mx(out=codes.bitcast(FP8X4), scales=scales, in_=values)
+
+        def cast_k(h):
+            nc.vector.tensor_copy(
+                out=k_bf[h][:].rearrange("p r s j -> p s j r"),
+                in_=k_raw[h][:].rearrange("p j (s r) -> p s j r", r=PACK),
+            )
+
+        def quantize_k(h):
+            cols = slice(64 * h, 64 * (h + 1))
+            for r in range(PACK):
+                quantize(k_codes[:, r, cols], k_scales[:, r, cols], k_bf[h][:, r].rearrange("p s j -> p (s j)"))
+
+        def cast_q(i, copy):
+            interleave(copy, q_bf[i][:], q_source(i))
+
+        def quantize_q(i):
+            quantize(q_codes[i][:], q_scales[i][:], q_bf[i][:].rearrange("p q j -> p (q j)"))
+
+        def score(n):
+            i, g = divmod(n, KV)
+            rows = slice(ROWS * g, ROWS * (g + 1))
+            for r in range(PACK):
+                nc.tensor.matmul_mx(
+                    out=scores[g][i % 2][:, r, :],
+                    lhsT=k_codes[rows, r, :].bitcast(FP8X4),
+                    lhsT_scale=k_scales[rows, r, :],
+                    rhs=q_codes[i][rows, :].bitcast(FP8X4),
+                    rhs_scale=q_scales[i][rows, :],
+                    start=True,
+                    stop=True,
+                )
+
+        def cap(n):
+            i, g = divmod(n, KV)
+            nc.scalar.activation(
+                out=capped[n][:], in_=scores[g][i % 2][:].rearrange("p r q -> p q r"), func=ACT.Tanh, scale=1.0 / CAP
+            )
+
+        def weigh(n):
+            nc.scalar.activation(out=prob[n][:], in_=capped[n][:], func=ACT.Sigmoid, scale=CAP)
+
+        def make_gate(i):
+            nc.scalar.activation(out=gate[i][:], in_=og_source(i), func=ACT.Sigmoid)
+
+        def scale_w(n):
+            nc.vector.tensor_tensor(
+                out=w_bf[n][:], in0=prob[n][:], in1=t_sb[:].unsqueeze(1).to_broadcast([P, QT, PACK]), op=ALU.mult
+            )
+
+        def quantize_w(n):
+            quantize(w_codes[n][:], w_scales[n][:], w_bf[n][:].rearrange("p q r -> p (q r)"))
+
+        def mix(n):
+            i, g = divmod(n, KV)
+            nc.tensor.matmul_mx(
+                out=y_banks[i % 4][:, i // 4, g, :],
+                lhsT=w_codes[n][:].bitcast(FP8X4),
+                lhsT_scale=w_scales[n][:],
+                rhs=v_codes[:, g, :].bitcast(FP8X4),
+                rhs_scale=v_scales[:, g, :],
+                start=True,
+                stop=True,
+            )
+
+        def finish(i):
+            nc.vector.scalar_tensor_tensor(
+                out=result[i][:], in0=y_banks[i % 4][:, i // 4], scalar=1.0 / 16.0, in1=gate[i][:],
+                op0=ALU.mult, op1=ALU.mult,
+            )
+            first, last = HEAD_SETS[i // TILES]
+            nc.sync.dma_start(out=out_hbm[:, first : last + 1 : last - first, i % TILES, :], in_=result[i][:])
+
+        make_gate(0)
+        cast_k(0)
+        quantize_k(0)
+        cast_k(1)
+        cast_q(0, nc.scalar.copy)
+        quantize_k(1)
+        quantize_q(0)
+        score(0)
+        score(1)
+        cast_q(1, nc.vector.tensor_copy)
+        cap(0)
+        quantize_q(1)
+        score(2)
+        score(3)
+        for g in range(KV):
+            interleave(nc.vector.tensor_copy, v_bf[:, g], v_raw[:, g])
+        quantize(
+            v_codes[:].rearrange("p g e -> p (g e)"),
+            v_scales[:].rearrange("p g e -> p (g e)"),
+            v_bf[:].rearrange("p g e j -> p (g e j)"),
+        )
+
+        late_gates = 2
+        for n in range(UNITS):
+            i, g = divmod(n, KV)
+            if n + 1 < UNITS:
+                cap(n + 1)
+            weigh(n)
+            if g == 0 and 1 <= i + 1 < PAIRS - late_gates:
+                make_gate(i + 1)
+            if n == UNITS - 1:
+                for late in range(PAIRS - late_gates, PAIRS):
+                    make_gate(late)
+            scale_w(n)
+            if g == 0:
+                if i + 2 < PAIRS:
+                    cast_q(i + 2, nc.vector.tensor_copy)
+                quantize_w(n)
+                mix(n)
+                if i + 2 < PAIRS:
+                    quantize_q(i + 2)
+                    score(n + 4)
+            else:
+                if i + 2 < PAIRS:
+                    score(n + 4)
+                if i >= 1:
+                    finish(i - 1)
+                quantize_w(n)
+                mix(n)
+        finish(PAIRS - 1)

@@ -37,9 +37,8 @@ def tile_rows_a_sigmoid_cap_gate_kernel(tc, qT, kT, t, v, og, out):
         def banks(name, count, shape):
             return [ps.tile(shape, F32, name="%s%d" % (name, i)) for i in range(count)]
 
-        half = N // 2
-        k_raw = tiles(sb, "k_raw", 2, [P, PACK, half], F32)
-        k_bf = tiles(sb, "k_bf", 2, [P, PACK, half // PACK, PACK], BF16)
+        k_raw = sb.tile([P, PACK, N], F32, align_bytes=64)
+        k_bf = sb.tile([P, PACK, P, PACK], BF16, align_bytes=64)
         k_codes = sb.tile([P, PACK, P], U32, align_bytes=64)
         k_scales = sb.tile([P, PACK, P], U8, align_bytes=64)
         q_one = tiles(sb, "q_one", 2, [P, PACK, QT], F32)
@@ -52,15 +51,13 @@ def tile_rows_a_sigmoid_cap_gate_kernel(tc, qT, kT, t, v, og, out):
         v_codes = sb.tile([P, KV, E], U32, align_bytes=64)
         v_scales = sb.tile([P, KV, E], U8, align_bytes=64)
         t_sb = sb.tile([P, PACK], F32, align_bytes=64)
-        og_first = sb.tile([P, KV, E], F32, align_bytes=64)
-        og_a = sb.tile([P, KV, TILES - 1, E], F32, align_bytes=64)
-        og_b = sb.tile([P, KV, TILES, E], F32, align_bytes=64)
-        gate = tiles(sb, "gate", PAIRS, [P, KV, E], F32)
-        capped = tiles(sb, "capped", UNITS, [P, QT, PACK], F32)
-        prob = tiles(sb, "prob", UNITS, [P, QT, PACK], F32)
-        w_bf = tiles(sb, "w_bf", UNITS, [P, QT, PACK], BF16)
-        w_codes = tiles(sb, "w_codes", UNITS, [P, QT], U32)
-        w_scales = tiles(sb, "w_scales", UNITS, [P, QT], U8)
+        og_sb = tiles(sb, "og_sb", 2, [P, KV, TILES, E], F32)
+        gate = tiles(sb, "gate", 2, [P, KV, TILES, E], F32)
+        capped = tiles(sb, "capped", PAIRS, [P, KV, QT, PACK], F32)
+        prob = tiles(sb, "prob", PAIRS, [P, KV, QT, PACK], F32)
+        w_bf = tiles(sb, "w_bf", PAIRS, [P, KV, QT, PACK], BF16)
+        w_codes = tiles(sb, "w_codes", PAIRS, [P, KV, QT], U32)
+        w_scales = tiles(sb, "w_scales", PAIRS, [P, KV, QT], U8)
         result = tiles(sb, "result", PAIRS, [P, KV, E], F32)
         scores = [banks("scores%d_" % g, 2, [P, PACK, QT]) for g in range(KV)]
         y_banks = banks("y", 4, [P, 2, KV, E])
@@ -70,37 +67,36 @@ def tile_rows_a_sigmoid_cap_gate_kernel(tc, qT, kT, t, v, og, out):
         q_a = q_hbm[ROWS : 3 * ROWS]
         og_hbm = og.rearrange("h (c p) e -> p h c e", p=P)
         out_hbm = out.rearrange("h (c p) e -> p h c e", p=P)
-        nc.sync.dma_start(out=og_first[:], in_=og_hbm[:, 1:3, 0, :])
-        for h in range(2):
-            nc.sync.dma_start(out=k_raw[h][:], in_=k_hbm[:, :, half * h : half * (h + 1)])
-        for c in range(2):
-            nc.sync.dma_start(out=q_one[c][:], in_=q_a[:, :, QT * c : QT * (c + 1)])
-        nc.sync.dma_start(out=t_sb[:], in_=t.rearrange("(p j) o -> p (j o)", j=PACK))
-        nc.sync.dma_start(out=v_raw[:], in_=v.rearrange("g (p j) e -> p g j e", j=PACK))
-        nc.sync.dma_start(out=q_two[0][:], in_=q_a[:, :, 2 * QT :])
-        for g in range(KV):
-            nc.sync.dma_start(out=og_a[:, g], in_=og_hbm[:, HEAD_SETS[0][g], 1:, :])
-        for c in range(2):
+
+        def load_og(s, g, cs):
+            nc.sync.dma_start(out=og_sb[s][:, g, cs, :], in_=og_hbm[:, HEAD_SETS[s][g], cs, :])
+
+        def load_q_split(c):
             for g in range(KV):
                 head = HEAD_SETS[1][g]
                 nc.sync.dma_start(
                     out=q_two[1 + c][ROWS * g : ROWS * (g + 1)],
                     in_=q_hbm[ROWS * head : ROWS * (head + 1), :, 2 * QT * c : 2 * QT * (c + 1)],
                 )
+
+        load_og(0, 0, slice(0, 1))
+        nc.sync.dma_start(out=k_raw[:], in_=k_hbm)
+        nc.sync.dma_start(out=q_one[0][:], in_=q_a[:, :, 0:QT])
+        load_og(0, 1, slice(0, TILES))
+        nc.sync.dma_start(out=q_one[1][:], in_=q_a[:, :, QT : 2 * QT])
+        nc.sync.dma_start(out=q_two[0][:], in_=q_a[:, :, 2 * QT :])
+        nc.sync.dma_start(out=t_sb[:], in_=t.rearrange("(p j) o -> p (j o)", j=PACK))
+        nc.sync.dma_start(out=v_raw[:], in_=v.rearrange("g (p j) e -> p g j e", j=PACK))
+        load_q_split(0)
+        load_og(0, 0, slice(1, TILES))
+        load_q_split(1)
         for g in range(KV):
-            nc.sync.dma_start(out=og_b[:, g], in_=og_hbm[:, HEAD_SETS[1][g], :, :])
+            load_og(1, g, slice(0, TILES))
 
         def q_source(i):
             if i < 2:
                 return q_one[i][:]
             return q_two[i // 2 - 1][:, :, QT * (i % 2) : QT * (i % 2 + 1)]
-
-        def og_source(i):
-            if i == 0:
-                return og_first[:]
-            if i < TILES:
-                return og_a[:, :, i - 1, :]
-            return og_b[:, :, i - TILES, :]
 
         def interleave(copy, dst, src):
             copy(out=dst.rearrange("p (c i) j -> p c j i", i=4), in_=src.rearrange("p j (c i) -> p c j i", i=4))
@@ -108,16 +104,14 @@ def tile_rows_a_sigmoid_cap_gate_kernel(tc, qT, kT, t, v, og, out):
         def quantize(codes, scales, values):
             nc.vector.quantize_mx(out=codes.bitcast(FP8X4), scales=scales, in_=values)
 
-        def cast_k(h):
-            nc.vector.tensor_copy(
-                out=k_bf[h][:].rearrange("p r s j -> p s j r"),
-                in_=k_raw[h][:].rearrange("p j (s r) -> p s j r", r=PACK),
+        def cast_k(copy, first, last):
+            copy(
+                out=k_bf[:, :, first:last, :].rearrange("p r s j -> p s j r"),
+                in_=k_raw[:, :, PACK * first : PACK * last].rearrange("p j (s r) -> p s j r", r=PACK),
             )
 
-        def quantize_k(h):
-            cols = slice(64 * h, 64 * (h + 1))
-            for r in range(PACK):
-                quantize(k_codes[:, r, cols], k_scales[:, r, cols], k_bf[h][:, r].rearrange("p s j -> p (s j)"))
+        def quantize_k(r):
+            quantize(k_codes[:, r, :], k_scales[:, r, :], k_bf[:, r].rearrange("p s j -> p (s j)"))
 
         def cast_q(i, copy):
             interleave(copy, q_bf[i][:], q_source(i))
@@ -142,90 +136,127 @@ def tile_rows_a_sigmoid_cap_gate_kernel(tc, qT, kT, t, v, og, out):
         def cap(n):
             i, g = divmod(n, KV)
             nc.scalar.activation(
-                out=capped[n][:], in_=scores[g][i % 2][:].rearrange("p r q -> p q r"), func=ACT.Tanh, scale=1.0 / CAP
+                out=capped[i][:, g], in_=scores[g][i % 2][:].rearrange("p r q -> p q r"), func=ACT.Tanh, scale=1.0 / CAP
             )
 
-        def weigh(n):
-            nc.scalar.activation(out=prob[n][:], in_=capped[n][:], func=ACT.Sigmoid, scale=CAP)
+        def part(tile_list, units):
+            i, g = divmod(units[0], KV)
+            return tile_list[i][:, g : g + len(units)]
 
-        def make_gate(i):
-            nc.scalar.activation(out=gate[i][:], in_=og_source(i), func=ACT.Sigmoid)
+        def weigh(units):
+            nc.scalar.activation(out=part(prob, units), in_=part(capped, units), func=ACT.Sigmoid, scale=CAP)
 
-        def scale_w(n):
+        def make_gate(s, gs, cs):
+            nc.scalar.activation(out=gate[s][:, gs, cs, :], in_=og_sb[s][:, gs, cs, :], func=ACT.Sigmoid)
+
+        def scale_w(units):
             nc.vector.tensor_tensor(
-                out=w_bf[n][:], in0=prob[n][:], in1=t_sb[:].unsqueeze(1).to_broadcast([P, QT, PACK]), op=ALU.mult
+                out=part(w_bf, units).rearrange("p g q r -> p (g q) r"),
+                in0=part(prob, units).rearrange("p g q r -> p (g q) r"),
+                in1=t_sb[:].unsqueeze(1).to_broadcast([P, QT * len(units), PACK]),
+                op=ALU.mult,
             )
 
-        def quantize_w(n):
-            quantize(w_codes[n][:], w_scales[n][:], w_bf[n][:].rearrange("p q r -> p (q r)"))
-
-        def mix(n):
+        def y_place(n):
             i, g = divmod(n, KV)
-            nc.tensor.matmul_mx(
-                out=y_banks[i % 4][:, i // 4, g, :],
-                lhsT=w_codes[n][:].bitcast(FP8X4),
-                lhsT_scale=w_scales[n][:],
-                rhs=v_codes[:, g, :].bitcast(FP8X4),
-                rhs_scale=v_scales[:, g, :],
-                start=True,
-                stop=True,
-            )
+            if n == UNITS - 1:
+                return y_banks[0][:, 0, 0:1, :]
+            return y_banks[i % 4][:, i // 4, g : g + 1, :]
 
-        def finish(i):
+        def mix(units):
+            quantize(
+                part(w_codes, units).rearrange("p g q -> p (g q)"),
+                part(w_scales, units).rearrange("p g q -> p (g q)"),
+                part(w_bf, units).rearrange("p g q r -> p (g q r)"),
+            )
+            for n in units:
+                i, g = divmod(n, KV)
+                nc.tensor.matmul_mx(
+                    out=y_place(n)[:, 0, :],
+                    lhsT=w_codes[i][:, g, :].bitcast(FP8X4),
+                    lhsT_scale=w_scales[i][:, g, :],
+                    rhs=v_codes[:, g, :].bitcast(FP8X4),
+                    rhs_scale=v_scales[:, g, :],
+                    start=True,
+                    stop=True,
+                )
+
+        def finish(units):
+            i, g = divmod(units[0], KV)
+            s, c = divmod(i, TILES)
+            gs = slice(g, g + len(units))
+            y = y_place(units[0]) if len(units) == 1 else y_banks[i % 4][:, i // 4]
             nc.vector.scalar_tensor_tensor(
-                out=result[i][:], in0=y_banks[i % 4][:, i // 4], scalar=1.0 / 16.0, in1=gate[i][:],
+                out=part(result, units), in0=y, scalar=1.0 / 16.0, in1=gate[s][:, gs, c, :],
                 op0=ALU.mult, op1=ALU.mult,
             )
-            first, last = HEAD_SETS[i // TILES]
-            nc.sync.dma_start(out=out_hbm[:, first : last + 1 : last - first, i % TILES, :], in_=result[i][:])
+            first, last = HEAD_SETS[s]
+            nc.sync.dma_start(out=out_hbm[:, first : last + 1 : last - first, c, :][:, gs, :], in_=part(result, units))
 
-        make_gate(0)
-        cast_k(0)
+        both = slice(0, KV)
+        split = 72
+        make_gate(0, slice(0, 1), slice(0, 1))
+        cast_k(nc.vector.tensor_copy, 0, split)
+        cast_k(nc.scalar.copy, split, P)
+        cast_q(0, nc.vector.tensor_copy)
         quantize_k(0)
-        cast_k(1)
-        cast_q(0, nc.scalar.copy)
-        quantize_k(1)
         quantize_q(0)
+        for r in range(1, PACK):
+            quantize_k(r)
         score(0)
         score(1)
+        make_gate(0, slice(1, 2), slice(0, TILES))
         cast_q(1, nc.vector.tensor_copy)
         cap(0)
         quantize_q(1)
         score(2)
         score(3)
+        cast_q(2, nc.vector.tensor_copy)
+        cast_q(3, nc.vector.tensor_copy)
+        quantize_q(2)
+        quantize_q(3)
+        score(4)
         for g in range(KV):
             interleave(nc.vector.tensor_copy, v_bf[:, g], v_raw[:, g])
-        quantize(
-            v_codes[:].rearrange("p g e -> p (g e)"),
-            v_scales[:].rearrange("p g e -> p (g e)"),
-            v_bf[:].rearrange("p g e j -> p (g e j)"),
-        )
 
-        late_gates = 2
-        for n in range(UNITS):
-            i, g = divmod(n, KV)
-            if n + 1 < UNITS:
-                cap(n + 1)
-            weigh(n)
-            if g == 0 and 1 <= i + 1 < PAIRS - late_gates:
-                make_gate(i + 1)
-            if n == UNITS - 1:
-                for late in range(PAIRS - late_gates, PAIRS):
-                    make_gate(late)
-            scale_w(n)
-            if g == 0:
-                if i + 2 < PAIRS:
-                    cast_q(i + 2, nc.vector.tensor_copy)
-                quantize_w(n)
-                mix(n)
-                if i + 2 < PAIRS:
-                    quantize_q(i + 2)
-                    score(n + 4)
-            else:
-                if i + 2 < PAIRS:
-                    score(n + 4)
-                if i >= 1:
-                    finish(i - 1)
-                quantize_w(n)
-                mix(n)
-        finish(PAIRS - 1)
+        wide = PAIRS - 2
+        groups = [[2 * i, 2 * i + 1] for i in range(wide)] + [[n] for n in range(2 * wide, UNITS)]
+        capped_to = 0
+        for step, units in enumerate(groups):
+            while capped_to < min(units[-1] + 1, UNITS - 1):
+                capped_to += 1
+                cap(capped_to)
+                if capped_to % 2 == 1 and capped_to + 4 < UNITS:
+                    score(capped_to + 4)
+            weigh(units)
+            if step == 2:
+                make_gate(0, slice(0, 1), slice(1, TILES))
+            if step == 5:
+                make_gate(1, both, slice(0, 2))
+            if step == len(groups) - 1:
+                make_gate(1, both, slice(2, TILES))
+                scale_w(units)
+                mix(groups[step - 1])
+                mix(units)
+                break
+            ahead = step + 3
+            if 4 <= ahead < PAIRS:
+                cast_q(ahead, nc.vector.tensor_copy)
+            if step >= 1:
+                mix(groups[step - 1])
+            if 4 <= ahead < PAIRS:
+                quantize_q(ahead)
+            if ahead < PAIRS:
+                score(2 * ahead)
+            scale_w(units)
+            if step == 0:
+                quantize(
+                    v_codes[:].rearrange("p g e -> p (g e)"),
+                    v_scales[:].rearrange("p g e -> p (g e)"),
+                    v_bf[:].rearrange("p g e j -> p (g e j)"),
+                )
+            if 2 <= step < 8:
+                finish([2 * (step - 2), 2 * (step - 2) + 1])
+        finish([12, 13])
+        finish([14])
+        finish([15])

@@ -143,17 +143,21 @@ def tile_rows_a_sigmoid_cap_gate_kernel(tc, qT, kT, t, v, og, out):
             i, g = divmod(units[0], KV)
             return tile_list[i][:, g : g + len(units)]
 
-        def weigh(units):
-            nc.scalar.activation(out=part(prob, units), in_=part(capped, units), func=ACT.Sigmoid, scale=CAP)
+        def flat(tile_list, units, qs):
+            return part(tile_list, units).rearrange("p g q r -> p (g q) r")[:, qs, :]
+
+        def weigh(units, qs=slice(None)):
+            nc.scalar.activation(out=flat(prob, units, qs), in_=flat(capped, units, qs), func=ACT.Sigmoid, scale=CAP)
 
         def make_gate(s, gs, cs):
             nc.scalar.activation(out=gate[s][:, gs, cs, :], in_=og_sb[s][:, gs, cs, :], func=ACT.Sigmoid)
 
-        def scale_w(units):
+        def scale_w(units, qs=slice(None)):
+            weights = flat(w_bf, units, qs)
             nc.vector.tensor_tensor(
-                out=part(w_bf, units).rearrange("p g q r -> p (g q) r"),
-                in0=part(prob, units).rearrange("p g q r -> p (g q) r"),
-                in1=t_sb[:].unsqueeze(1).to_broadcast([P, QT * len(units), PACK]),
+                out=weights,
+                in0=flat(prob, units, qs),
+                in1=t_sb[:].unsqueeze(1).to_broadcast(weights.shape),
                 op=ALU.mult,
             )
 
@@ -194,7 +198,7 @@ def tile_rows_a_sigmoid_cap_gate_kernel(tc, qT, kT, t, v, og, out):
             nc.sync.dma_start(out=out_hbm[:, first : last + 1 : last - first, c, :][:, gs, :], in_=part(result, units))
 
         both = slice(0, KV)
-        split = 72
+        split = 80
         make_gate(0, slice(0, 1), slice(0, 1))
         cast_k(nc.vector.tensor_copy, 0, split)
         cast_k(nc.scalar.copy, split, P)
@@ -216,47 +220,63 @@ def tile_rows_a_sigmoid_cap_gate_kernel(tc, qT, kT, t, v, og, out):
         quantize_q(2)
         quantize_q(3)
         score(4)
+
+        cap(1)
+        score(5)
+        weigh([0])
+        scale_w([0])
         for g in range(KV):
             interleave(nc.vector.tensor_copy, v_bf[:, g], v_raw[:, g])
+        cap(2)
+        score(6)
+        weigh([1])
+        scale_w([1])
+        quantize(
+            v_codes[:].rearrange("p g e -> p (g e)"),
+            v_scales[:].rearrange("p g e -> p (g e)"),
+            v_bf[:].rearrange("p g e j -> p (g e j)"),
+        )
 
-        wide = PAIRS - 2
-        groups = [[2 * i, 2 * i + 1] for i in range(wide)] + [[n] for n in range(2 * wide, UNITS)]
-        capped_to = 0
-        for step, units in enumerate(groups):
-            while capped_to < min(units[-1] + 1, UNITS - 1):
-                capped_to += 1
-                cap(capped_to)
-                if capped_to % 2 == 1 and capped_to + 4 < UNITS:
-                    score(capped_to + 4)
+        for i in range(1, PAIRS - 2):
+            units = [2 * i, 2 * i + 1]
+            ahead = i + 3
+            cap(2 * i + 1)
+            score(2 * i + 5)
+            cap(2 * i + 2)
             weigh(units)
-            if step == 2:
+            if i == 2:
                 make_gate(0, slice(0, 1), slice(1, TILES))
-            if step == 5:
+            if i == PAIRS - 3:
                 make_gate(1, both, slice(0, 2))
-            if step == len(groups) - 1:
-                make_gate(1, both, slice(2, TILES))
-                scale_w(units)
-                mix(groups[step - 1])
-                mix(units)
-                break
-            ahead = step + 3
-            if 4 <= ahead < PAIRS:
-                cast_q(ahead, nc.vector.tensor_copy)
-            if step >= 1:
-                mix(groups[step - 1])
-            if 4 <= ahead < PAIRS:
-                quantize_q(ahead)
             if ahead < PAIRS:
+                cast_q(ahead, nc.vector.tensor_copy)
+            mix([2 * i - 2, 2 * i - 1])
+            if ahead < PAIRS:
+                quantize_q(ahead)
                 score(2 * ahead)
             scale_w(units)
-            if step == 0:
-                quantize(
-                    v_codes[:].rearrange("p g e -> p (g e)"),
-                    v_scales[:].rearrange("p g e -> p (g e)"),
-                    v_bf[:].rearrange("p g e j -> p (g e j)"),
-                )
-            if 2 <= step < 8:
-                finish([2 * (step - 2), 2 * (step - 2) + 1])
+            if i >= 2:
+                finish([2 * i - 4, 2 * i - 3])
+
+        cap(13)
+        weigh([12])
+        mix([10, 11])
+        scale_w([12])
+        finish([8, 9])
+        cap(14)
+        weigh([13])
+        mix([12])
+        scale_w([13])
+        finish([10, 11])
+        cap(15)
+        weigh([14])
+        mix([13])
+        scale_w([14])
+        weigh([15])
+        scale_w([15])
+        make_gate(1, both, slice(2, TILES))
+        for n in (14, 15):
+            mix([n])
         finish([12, 13])
         finish([14])
         finish([15])

from contextlib import ExitStack

import concourse.mybir as mybir

H, KV, D, NQ, N, E = 4, 2, 256, 512, 512, 128
CAP = 2.0
FLOPS = 2 * H * N * NQ * D + 2 * H * N * NQ * E

F32 = mybir.dt.float32
BF16 = mybir.dt.bfloat16
U32 = mybir.dt.uint32
U8 = mybir.dt.uint8
FP8X4 = mybir.dt.float8_e4m3fn_x4
ACT = mybir.ActivationFunctionType
ALU = mybir.AluOpType

P = 128
PACK = 4
ROWS = D // PACK
QT = 128
TILES = NQ // QT
HEAD_SETS = ((1, 2), (0, 3))
PAIRS = len(HEAD_SETS) * TILES
UNITS = KV * PAIRS


def tile_rows_a_sigmoid_cap_gate_kernel(tc, qT, kT, t, v, og, out):
    nc = tc.nc
    with ExitStack() as ctx:
        sb = ctx.enter_context(tc.tile_pool(name="sb", bufs=1))
        ps = ctx.enter_context(tc.psum_pool(name="ps", bufs=1))
        ctx.enter_context(tc.manual_schedule())

        def tiles(pool, name, count, shape, dtype):
            return [pool.tile(shape, dtype, name="%s%d" % (name, i), align_bytes=64) for i in range(count)]

        def banks(name, count, shape):
            return [ps.tile(shape, F32, name="%s%d" % (name, i)) for i in range(count)]

        k_raw = sb.tile([P, PACK, N], F32, align_bytes=64)
        k_bf = sb.tile([P, PACK, P, PACK], BF16, align_bytes=64)
        k_codes = sb.tile([P, PACK, P], U32, align_bytes=64)
        k_scales = sb.tile([P, PACK, P], U8, align_bytes=64)
        q_one = tiles(sb, "q_one", 2, [P, PACK, QT], F32)
        q_two = tiles(sb, "q_two", 3, [P, PACK, 2 * QT], F32)
        q_bf = tiles(sb, "q_bf", PAIRS, [P, QT, PACK], BF16)
        q_codes = tiles(sb, "q_codes", PAIRS, [P, QT], U32)
        q_scales = tiles(sb, "q_scales", PAIRS, [P, QT], U8)
        v_raw = sb.tile([P, KV, PACK, E], F32, align_bytes=64)
        v_bf = sb.tile([P, KV, E, PACK], BF16, align_bytes=64)
        v_codes = sb.tile([P, KV, E], U32, align_bytes=64)
        v_scales = sb.tile([P, KV, E], U8, align_bytes=64)
        t_sb = sb.tile([P, PACK], F32, align_bytes=64)
        og_sb = tiles(sb, "og_sb", 2, [P, KV, TILES, E], F32)
        gate = tiles(sb, "gate", 2, [P, KV, TILES, E], F32)
        capped = tiles(sb, "capped", PAIRS, [P, KV, QT, PACK], F32)
        prob = tiles(sb, "prob", PAIRS, [P, KV, QT, PACK], F32)
        w_bf = tiles(sb, "w_bf", PAIRS, [P, KV, QT, PACK], BF16)
        w_codes = tiles(sb, "w_codes", PAIRS, [P, KV, QT], U32)
        w_scales = tiles(sb, "w_scales", PAIRS, [P, KV, QT], U8)
        result = tiles(sb, "result", PAIRS, [P, KV, E], F32)
        scores = [banks("scores%d_" % g, 2, [P, PACK, QT]) for g in range(KV)]
        y_banks = banks("y", 4, [P, 2, KV, E])

        k_hbm = kT.rearrange("g (p j) n -> (g p) j n", j=PACK)
        q_hbm = qT.rearrange("h (p j) n -> (h p) j n", j=PACK)
        q_a = q_hbm[ROWS : 3 * ROWS]
        og_hbm = og.rearrange("h (c p) e -> p h c e", p=P)
        out_hbm = out.rearrange("h (c p) e -> p h c e", p=P)

        def load_og(s, g, cs):
            nc.sync.dma_start(out=og_sb[s][:, g, cs, :], in_=og_hbm[:, HEAD_SETS[s][g], cs, :])

        def load_q_split(c):
            for g in range(KV):
                head = HEAD_SETS[1][g]
                nc.sync.dma_start(
                    out=q_two[1 + c][ROWS * g : ROWS * (g + 1)],
                    in_=q_hbm[ROWS * head : ROWS * (head + 1), :, 2 * QT * c : 2 * QT * (c + 1)],
                )

        load_og(0, 0, slice(0, 1))
        nc.sync.dma_start(out=k_raw[:], in_=k_hbm)
        nc.sync.dma_start(out=q_one[0][:], in_=q_a[:, :, 0:QT])
        load_og(0, 1, slice(0, TILES))
        nc.sync.dma_start(out=q_one[1][:], in_=q_a[:, :, QT : 2 * QT])
        nc.sync.dma_start(out=q_two[0][:], in_=q_a[:, :, 2 * QT :])
        nc.sync.dma_start(out=t_sb[:], in_=t.rearrange("(p j) o -> p (j o)", j=PACK))
        nc.sync.dma_start(out=v_raw[:], in_=v.rearrange("g (p j) e -> p g j e", j=PACK))
        load_q_split(0)
        load_og(0, 0, slice(1, TILES))
        load_q_split(1)
        for g in range(KV):
            load_og(1, g, slice(0, TILES))

        def q_source(i):
            if i < 2:
                return q_one[i][:]
            return q_two[i // 2 - 1][:, :, QT * (i % 2) : QT * (i % 2 + 1)]

        def interleave(copy, dst, src):
            copy(out=dst.rearrange("p (c i) j -> p c j i", i=4), in_=src.rearrange("p j (c i) -> p c j i", i=4))

        def quantize(codes, scales, values):
            nc.vector.quantize_mx(out=codes.bitcast(FP8X4), scales=scales, in_=values)

        def cast_k(copy, first, last):
            copy(
                out=k_bf[:, :, first:last, :].rearrange("p r s j -> p s j r"),
                in_=k_raw[:, :, PACK * first : PACK * last].rearrange("p j (s r) -> p s j r", r=PACK),
            )

        def quantize_k(r):
            quantize(k_codes[:, r, :], k_scales[:, r, :], k_bf[:, r].rearrange("p s j -> p (s j)"))

        def cast_q(i, copy):
            interleave(copy, q_bf[i][:], q_source(i))

        def quantize_q(i):
            quantize(q_codes[i][:], q_scales[i][:], q_bf[i][:].rearrange("p q j -> p (q j)"))

        def score(n):
            i, g = divmod(n, KV)
            rows = slice(ROWS * g, ROWS * (g + 1))
            for r in range(PACK):
                nc.tensor.matmul_mx(
                    out=scores[g][i % 2][:, r, :],
                    lhsT=k_codes[rows, r, :].bitcast(FP8X4),
                    lhsT_scale=k_scales[rows, r, :],
                    rhs=q_codes[i][rows, :].bitcast(FP8X4),
                    rhs_scale=q_scales[i][rows, :],
                    start=True,
                    stop=True,
                )

        def cap(n):
            i, g = divmod(n, KV)
            nc.scalar.activation(
                out=capped[i][:, g], in_=scores[g][i % 2][:].rearrange("p r q -> p q r"), func=ACT.Tanh, scale=1.0 / CAP
            )

        def part(tile_list, units):
            i, g = divmod(units[0], KV)
            return tile_list[i][:, g : g + len(units)]

        def flat(tile_list, units, qs):
            return part(tile_list, units).rearrange("p g q r -> p (g q) r")[:, qs, :]

        def weigh(units, qs=slice(None)):
            nc.scalar.activation(out=flat(prob, units, qs), in_=flat(capped, units, qs), func=ACT.Sigmoid, scale=CAP)

        def make_gate(s, gs, cs):
            nc.scalar.activation(out=gate[s][:, gs, cs, :], in_=og_sb[s][:, gs, cs, :], func=ACT.Sigmoid)

        def scale_w(units, qs=slice(None)):
            weights = flat(w_bf, units, qs)
            nc.vector.tensor_tensor(
                out=weights,
                in0=flat(prob, units, qs),
                in1=t_sb[:].unsqueeze(1).to_broadcast(weights.shape),
                op=ALU.mult,
            )

        def y_place(n):
            i, g = divmod(n, KV)
            if n == UNITS - 1:
                return y_banks[0][:, 0, 0:1, :]
            return y_banks[i % 4][:, i // 4, g : g + 1, :]

        def mix(units):
            quantize(
                part(w_codes, units).rearrange("p g q -> p (g q)"),
                part(w_scales, units).rearrange("p g q -> p (g q)"),
                part(w_bf, units).rearrange("p g q r -> p (g q r)"),
            )
            for n in units:
                i, g = divmod(n, KV)
                nc.tensor.matmul_mx(
                    out=y_place(n)[:, 0, :],
                    lhsT=w_codes[i][:, g, :].bitcast(FP8X4),
                    lhsT_scale=w_scales[i][:, g, :],
                    rhs=v_codes[:, g, :].bitcast(FP8X4),
                    rhs_scale=v_scales[:, g, :],
                    start=True,
                    stop=True,
                )

        def finish(units):
            i, g = divmod(units[0], KV)
            s, c = divmod(i, TILES)
            gs = slice(g, g + len(units))
            y = y_place(units[0]) if len(units) == 1 else y_banks[i % 4][:, i // 4]
            nc.vector.scalar_tensor_tensor(
                out=part(result, units), in0=y, scalar=1.0 / 16.0, in1=gate[s][:, gs, c, :],
                op0=ALU.mult, op1=ALU.mult,
            )
            first, last = HEAD_SETS[s]
            nc.sync.dma_start(out=out_hbm[:, first : last + 1 : last - first, c, :][:, gs, :], in_=part(result, units))

        both = slice(0, KV)
        split = 80
        make_gate(0, slice(0, 1), slice(0, 1))
        cast_k(nc.vector.tensor_copy, 0, split)
        cast_k(nc.scalar.copy, split, P)
        cast_q(0, nc.vector.tensor_copy)
        quantize_k(0)
        quantize_q(0)
        for r in range(1, PACK):
            quantize_k(r)
        score(0)
        score(1)
        make_gate(0, slice(1, 2), slice(0, TILES))
        cast_q(1, nc.vector.tensor_copy)
        cap(0)
        quantize_q(1)
        score(2)
        score(3)
        cast_q(2, nc.vector.tensor_copy)
        cast_q(3, nc.vector.tensor_copy)
        quantize_q(2)
        quantize_q(3)
        score(4)

        cap(1)
        score(5)
        weigh([0])
        scale_w([0])
        for g in range(KV):
            interleave(nc.vector.tensor_copy, v_bf[:, g], v_raw[:, g])
        cap(2)
        score(6)
        weigh([1])
        scale_w([1])
        quantize(
            v_codes[:].rearrange("p g e -> p (g e)"),
            v_scales[:].rearrange("p g e -> p (g e)"),
            v_bf[:].rearrange("p g e j -> p (g e j)"),
        )

        for i in range(1, PAIRS - 2):
            units = [2 * i, 2 * i + 1]
            ahead = i + 3
            cap(2 * i + 1)
            score(2 * i + 5)
            cap(2 * i + 2)
            weigh(units)
            if i == 2:
                make_gate(0, slice(0, 1), slice(1, TILES))
            if i == PAIRS - 3:
                make_gate(1, both, slice(0, 2))
            if ahead < PAIRS:
                cast_q(ahead, nc.vector.tensor_copy)
            mix([2 * i - 2, 2 * i - 1])
            if ahead < PAIRS:
                quantize_q(ahead)
                score(2 * ahead)
            scale_w(units)
            if i >= 2:
                finish([2 * i - 4, 2 * i - 3])

        cap(13)
        weigh([12])
        mix([10, 11])
        scale_w([12])
        finish([8, 9])
        cap(14)
        weigh([13])
        mix([12])
        scale_w([13])
        finish([10, 11])
        cap(15)
        weigh([14])
        mix([13])
        scale_w([14])
        weigh([15])
        scale_w([15])
        make_gate(1, both, slice(2, TILES))
        for n in (14, 15):
            mix([n])
        finish([12, 13])
        finish([14])
        finish([15])
